import numpy as np
import ml_dtypes


def mxq(x, axis, fmt="e4m3"):
    dtype, down = {"e4m3": (ml_dtypes.float8_e4m3fn, 7), "e5m2": (ml_dtypes.float8_e5m2, 14)}[fmt]
    v = np.moveaxis(np.asarray(x, np.float32).astype(ml_dtypes.bfloat16).astype(np.float64), axis, -1)
    blocks = v.reshape(v.shape[:-1] + (-1, 32))
    amax = np.abs(blocks).max(-1, keepdims=True)
    byte = np.maximum(np.where(amax > 0, np.frexp(amax)[1] - 1 + 127, 0) - down, 1)
    scale = np.exp2(byte - 127.0)
    codes = (blocks / scale).astype(np.float32).astype(dtype).astype(np.float64)
    return np.moveaxis((codes * scale).reshape(v.shape), -1, axis)


WIDE = False


def mx_kscale(k):
    if not WIDE:
        return np.ones(k)
    levels = np.array([10, -10, 5, -5, 0])
    if k % 512:
        return np.exp2(np.random.permutation(np.resize(levels, k // 32))).repeat(32)
    a = np.empty((k // 512, 16))
    for p in range(k // 512):
        a[p, :8] = np.random.permutation(np.resize(levels, 8))
        for g in range(8):
            far = levels[np.abs(levels - a[p, g]) >= 10]
            a[p, g + 8] = far[np.random.randint(len(far))]
    return np.exp2(a.ravel()).repeat(32)


def f64(x):
    return np.asarray(x).astype(np.float64)


def striped(idx):
    return np.tile(idx.reshape(-1, 16).T, (8, 1)).astype(np.uint16)


def unstriped(offs):
    return offs[:16].T.reshape(-1).astype(np.int64)


def pack_weight(w):
    k, n = w.shape
    w = f64(np.asarray(w, np.float32).astype(ml_dtypes.bfloat16)).reshape(k // 32, 32, n)
    amax = np.abs(w).max(1)
    byte = np.clip(np.where(amax > 0, np.frexp(amax)[1] - 1 + 127 - 7, 1), 1, 254)
    scaled = (w * np.exp2(127.0 - byte)[:, None, :]).reshape(k, n).astype(np.float32)
    words = np.ascontiguousarray(scaled.reshape(k // 512, 128, 4, n).transpose(0, 1, 3, 2)).astype(ml_dtypes.float8_e4m3fn).view(np.uint8)
    return words, np.ascontiguousarray(byte.astype(np.uint8).reshape(k // 512, 16, n))


def unpack_weight(words, scales):
    g, p, n, _ = words.shape
    vals = np.ascontiguousarray(words).view(ml_dtypes.float8_e4m3fn).astype(np.float64) * np.repeat(np.exp2(scales.astype(np.float64) - 127.0), 8, axis=1)[..., None]
    return vals.transpose(0, 1, 3, 2).reshape(g * 512, n)


K, T, S, V, D, W = 512, 2048, 512, 512, 8, 2048


def setup_inputs():
    n = np.random.standard_normal
    s = mx_kscale(K)[:, None]
    packed_xT = pack_weight(n((K, T)) * s)
    packed_eT = pack_weight(n((K, W)) * s)
    return {
        "x_words": packed_xT[0],
        "x_scales": packed_xT[1],
        "e_words": packed_eT[0],
        "e_scales": packed_eT[1],
        "wq": (n((K, V)) / np.sqrt(K) / s).astype(np.float32),
        "wh": (n((K, V)) / np.sqrt(K) / s).astype(np.float32),
        "wo": (n((K, V)) / np.sqrt(K) / s).astype(np.float32),
        "offs": striped(np.random.permutation(T)[:S]),
        "obs": striped(np.random.permutation(W)[:S]),
    }


def reference(x_words, x_scales, e_words, e_scales, wq, wh, wo, offs, obs):
    xq = unpack_weight(x_words, x_scales)[:, unstriped(offs)]
    whq = mxq(f64(wh), 0, "e4m3")
    e_obs = unpack_weight(e_words, e_scales)[:, unstriped(obs)]
    woq = mxq(f64(wo), 0, "e4m3")
    z = xq.T @ whq + e_obs.T @ woq
    eq = np.exp(z)
    sq = eq.reshape(len(eq), -1, D).sum(axis=2)
    q1 = 0.99 * (eq / np.repeat(sq, D, axis=1)) + 0.00125
    wqq = mxq(f64(wq), 0, "e4m3")
    y = xq.T @ wqq
    ep = np.exp(y)
    sp = ep.reshape(len(ep), -1, D).sum(axis=2)
    p1 = 0.99 * (ep / np.repeat(sp, D, axis=1)) + 0.00125
    kl = q1 * (np.log(q1) - np.log(p1))
    return kl.reshape(len(kl), -1, D).sum(axis=2)

@@ -1,0 +1,254 @@
+from contextlib import ExitStack
+
+import concourse.mybir as mybir
+from concourse.masks import make_identity
+
+F32 = mybir.dt.float32
+BF16 = mybir.dt.bfloat16
+I32 = mybir.dt.int32
+U32 = mybir.dt.uint32
+U16 = mybir.dt.uint16
+U8 = mybir.dt.uint8
+FP8X4 = mybir.dt.float8_e4m3fn_x4
+ALU = mybir.AluOpType
+ACT = mybir.ActivationFunctionType
+AXIS = mybir.AxisListType
+
+P = 128
+PACK = 4
+K = 512
+STORE = 2048
+STEPS = 512
+LOGITS = 512
+CLASSES = 8
+HALVES = 2
+HALF = LOGITS // HALVES
+GROUPS = HALF // CLASSES
+BLOCKS = STEPS // P
+KEEP = 0.99
+FLOOR = 0.00125
+MIX = FLOOR / KEEP
+
+FLOPS = 2 * 3 * STEPS * K * LOGITS
+
+
+def tile_picked_ydream_kl_p_kernel(
+    tc, x_words, x_scales, e_words, e_scales, wq, wh, wo, offs, obs, out
+):
+    nc = tc.nc
+    with ExitStack() as ctx:
+        keep = ctx.enter_context(tc.tile_pool(name="keep", bufs=1))
+        psum = ctx.enter_context(tc.psum_pool(name="psum", bufs=1))
+
+        def load_list(src, name):
+            t = keep.tile([P, STEPS // 16], U16, name=name)
+            nc.sync.dma_start(t[:], src)
+            return t
+
+        def load_scales(src, name, queue):
+            t = keep.tile([P, STORE], U8, name=name, align_bytes=64)
+            nc.vector.memset(t[:].bitcast(I32), 0)
+            for q in range(4):
+                queue.dma_start(
+                    out=t[32 * q : 32 * q + 4, :].bitcast(I32),
+                    in_=src[0, 4 * q : 4 * q + 4, :].bitcast(I32),
+                )
+            return t
+
+        def load_words(src, name):
+            t = keep.tile([P, STORE], I32, name=name, align_bytes=64)
+            nc.sync.dma_start(out=t[:], in_=src[0].rearrange("p n t -> p (n t)").bitcast(I32))
+            return t
+
+        def load_weight(w, h, name):
+            t = keep.tile([P, PACK, HALF], F32, name=name, tag=name, align_bytes=64)
+            nc.sync.dma_start(
+                out=t[:], in_=w[:, h * HALF : (h + 1) * HALF].rearrange("(p j) c -> p j c", j=PACK)
+            )
+            return t
+
+        def pick_codes(words, lst, name):
+            codes = keep.tile([P, STEPS], U32, name=name + "_codes", align_bytes=64)
+            nc.vector.tensor_copy(codes[:], words[:].bitcast(U32).indirect(lst[:]))
+            return codes
+
+        def pick_scales(scales, lst, name):
+            exps = keep.tile([P, STEPS], U8, name=name + "_exps", align_bytes=64)
+            nc.vector.tensor_copy(exps[:], scales[:].indirect(lst[:]))
+            return exps
+
+        def interleave(raw, name):
+            grouped = keep.tile([P, HALF, PACK], BF16, name=name + "_bf", align_bytes=64)
+            nc.scalar.copy(
+                out=grouped[:].rearrange("p (c i) j -> p c j i", i=4),
+                in_=raw[:].rearrange("p j (c i) -> p c j i", i=4),
+            )
+            return grouped
+
+        def quantise(grouped, name):
+            codes = keep.tile([P, HALF], U32, name=name + "_codes", align_bytes=64)
+            exps = keep.tile([P, HALF], U8, name=name + "_exps", align_bytes=64)
+            nc.vector.quantize_mx(
+                out=codes[:].bitcast(FP8X4), scales=exps[:], in_=grouped[:].rearrange("p c j -> p (c j)")
+            )
+            return codes, exps
+
+        def logits(pairs, name):
+            banks = []
+            for b in range(BLOCKS // 2):
+                bank = psum.tile([P, 2, HALF], F32, name=name + "_bank%d" % b, tag="logits", bufs=4)
+                for i in range(2):
+                    rows = slice((2 * b + i) * P, (2 * b + i + 1) * P)
+                    for n, ((a_codes, a_exps), (w_codes, w_exps)) in enumerate(pairs):
+                        nc.tensor.matmul_mx(
+                            out=bank[:, i, :],
+                            lhsT=a_codes[:, rows].bitcast(FP8X4),
+                            lhsT_scale=a_exps[:, rows],
+                            rhs=w_codes[:].bitcast(FP8X4),
+                            rhs_scale=w_exps[:],
+                            start=(n == 0),
+                            stop=(n == len(pairs) - 1),
+                        )
+                banks.append(bank)
+            return banks
+
+        def exp_shifted(banks, name, tag, exp_tag):
+            t = keep.tile([P, CLASSES, P], F32, name=name + "_shift", tag=tag)
+            e = keep.tile([P, CLASSES, P], F32, name=name + "_exp", tag=exp_tag, align_bytes=64)
+            for b, bank in enumerate(banks):
+                top = keep.tile([P, 2 * GROUPS], F32, name=name + "_top%d" % b)
+                nc.vector.tensor_reduce(
+                    out=top[:],
+                    in_=bank[:].rearrange("p i (g d) -> p (i g) d", d=CLASSES),
+                    axis=AXIS.X,
+                    op=ALU.max,
+                )
+                nc.vector.tensor_tensor(
+                    out=t[:, :, b * 2 * GROUPS : (b + 1) * 2 * GROUPS],
+                    in0=bank[:].rearrange("p i (g d) -> p d (i g)", d=CLASSES),
+                    in1=top[:].unsqueeze(1).to_broadcast([P, CLASSES, 2 * GROUPS]),
+                    op=ALU.subtract,
+                )
+                cols = slice(b * 2 * GROUPS, (b + 1) * 2 * GROUPS)
+                nc.scalar.activation(out=e[:, :, cols], in_=t[:, :, cols], func=ACT.Exp)
+            return e
+
+        def turn_sum(acc, parts, start, stop):
+            for n, part in enumerate(parts):
+                nc.tensor.matmul(
+                    out=acc,
+                    lhsT=part,
+                    rhs=ident[:],
+                    is_transpose=True,
+                    start=start and n == 0,
+                    stop=stop and n == len(parts) - 1,
+                )
+
+        def class_sums(e, mix_t, name, early):
+            total = psum.tile([P, P], F32, name=name + "_total", tag="total")
+            turn_sum(total[:], [e[:, d, :] for d in range(CLASSES)], True, True)
+            if early:
+                nc.scalar.activation(out=mix_t, in_=total[:], func=ACT.Copy, scale=MIX)
+            else:
+                nc.vector.tensor_scalar(out=mix_t, in0=total[:], scalar1=MIX, scalar2=None, op0=ALU.mult)
+            back = psum.tile([P, P], F32, name=name + "_back", tag="back")
+            nc.tensor.transpose(back[:], mix_t, ident[:])
+            return back
+
+        def mixed(engine, e, addend, name):
+            a = keep.tile([P, CLASSES, P], F32, name=name + "_mixed")
+            engine.tensor_tensor(
+                out=a[:],
+                in0=e[:],
+                in1=addend[:].unsqueeze(1).to_broadcast([P, CLASSES, P]),
+                op=ALU.add,
+            )
+            return a
+
+        x_list = load_list(offs, "x_list")
+        xs = load_scales(x_scales, "xs", nc.scalar)
+        wq_raw = [load_weight(wq, 0, "wq0")]
+        xw = load_words(x_words, "xw")
+        wq_raw.append(load_weight(wq, 1, "wq1"))
+        e_list = load_list(obs, "e_list")
+        es = load_scales(e_scales, "es", nc.gpsimd)
+        ew = load_words(e_words, "ew")
+        wz_raw = [(load_weight(wh, h, "wh%d" % h), load_weight(wo, h, "wo%d" % h)) for h in range(HALVES)]
+
+        ident = keep.tile([P, P], F32, name="ident")
+        make_identity(nc, ident[:])
+
+        mix = keep.tile([P, 2, HALVES, P], F32, name="mix")
+
+        x_exps = pick_scales(xs, x_list, "x")
+        x = (pick_codes(xw, x_list, "x"), x_exps)
+        e_exps = pick_scales(es, e_list, "e")
+        wq_bf = [interleave(wq_raw[h], "wq%d" % h) for h in range(HALVES)]
+        wz_bf = [(interleave(wz_raw[h][0], "wh%d" % h), interleave(wz_raw[h][1], "wo%d" % h)) for h in range(HALVES)]
+        prior = []
+        for h in range(HALVES):
+            name = "y%d" % h
+            w = quantise(wq_bf[h], "wq%d" % h)
+            y_exp = exp_shifted(logits([(x, w)], name), name, name, "wo1" if h else "wq0")
+            back = class_sums(y_exp, mix[:, 0, h, :], name, True)
+            addend = keep.tile([P, P], F32, name=name + "_addend")
+            nc.scalar.copy(out=addend[:], in_=back[:])
+            prior.append(mixed(nc.gpsimd, y_exp, addend, name))
+        e = (pick_codes(ew, e_list, "e"), e_exps)
+        wz = [(quantise(wz_bf[h][0], "wh%d" % h), quantise(wz_bf[h][1], "wo%d" % h)) for h in range(HALVES)]
+        z_exp = [
+            exp_shifted(logits([(x, wz[h][0]), (e, wz[h][1])], "z%d" % h), "z%d" % h, "z%d" % h, "wh%d" % h)
+            for h in range(HALVES)
+        ]
+        post = []
+        inv = keep.tile([P, HALVES, P], F32, name="inv")
+        for h in range(HALVES):
+            back = class_sums(z_exp[h], mix[:, 1, h, :], "z%d" % h, False)
+            post.append(mixed(nc.vector, z_exp[h], back, "z%d" % h))
+        nc.vector.reciprocal(out=inv[:, 0, :], in_=mix[:, 1, 0, :])
+
+        logs = keep.tile([P, 2 * HALVES * CLASSES + 2 * HALVES, P], F32, name="logs", tag="z%d" % (HALVES - 1))
+        sums = []
+        for h in range(HALVES):
+            ln_b = logs[:, h * CLASSES : (h + 1) * CLASSES, :]
+            nc.scalar.activation(out=ln_b, in_=prior[h][:], func=ACT.Ln)
+            cross = keep.tile([P, CLASSES * P], F32, name="cross%d" % h)
+            nc.vector.scalar_tensor_tensor(
+                out=cross[:],
+                in0=ln_b.rearrange("p d c -> p (d c)"),
+                scalar=-1.0,
+                in1=post[h][:].rearrange("p d c -> p (d c)"),
+                op0=ALU.mult,
+                op1=ALU.mult,
+            )
+            acc = psum.tile([P, P], F32, name="acc%d" % h)
+            turn_sum(acc[:], [cross[:, d * P : (d + 1) * P] for d in range(CLASSES)], True, False)
+            sums.append(acc)
+
+        for h in range(HALVES):
+            ln_a = logs[:, (HALVES + h) * CLASSES : (HALVES + h + 1) * CLASSES, :]
+            own = keep.tile([P, CLASSES, P], F32, name="own%d" % h)
+            for part in range(2):
+                ds = slice(part * CLASSES // 2, (part + 1) * CLASSES // 2)
+                nc.scalar.activation(out=ln_a[:, ds], in_=post[h][:, ds], func=ACT.Ln)
+                nc.vector.tensor_tensor(out=own[:, ds], in0=ln_a[:, ds], in1=post[h][:, ds], op=ALU.mult)
+            turn_sum(sums[h][:], [own[:, d, :] for d in range(CLASSES)], False, True)
+
+        nc.vector.reciprocal(out=inv[:, 1, :], in_=mix[:, 1, 1, :])
+        ln_mix = logs[:, 2 * HALVES * CLASSES :, :]
+        nc.scalar.activation(out=ln_mix, in_=mix[:].rearrange("p s h c -> p (s h) c"), func=ACT.Ln)
+        gap = keep.tile([P, HALVES, P], F32, name="gap")
+        nc.gpsimd.tensor_tensor(out=gap[:], in0=ln_mix[:, :HALVES], in1=ln_mix[:, HALVES:], op=ALU.subtract)
+
+        for h in range(HALVES):
+            scaled = keep.tile([P, P], F32, name="scaled%d" % h)
+            nc.vector.scalar_tensor_tensor(
+                out=scaled[:], in0=sums[h][:], scalar=FLOOR, in1=inv[:, h, :], op0=ALU.mult, op1=ALU.mult
+            )
+            res = psum.tile([P, P], F32, name="res%d" % h, tag="back" if h else "total")
+            turn_sum(res[:], [gap[:, h, :], scaled[:]], True, True)
+            staged = keep.tile([P, BLOCKS, GROUPS], F32, name="staged%d" % h)
+            nc.vector.tensor_copy(out=staged[:].rearrange("p b g -> p (b g)"), in_=res[:])
+            nc.sync.dma_start(
+                out=out[:, h * GROUPS : (h + 1) * GROUPS].rearrange("(b p) g -> p b g", p=P), in_=staged[:]
+            )

@@ -21,10 +21,9 @@ STORE = 2048
 STEPS = 512
 LOGITS = 512
 CLASSES = 8
-HALVES = 2
-HALF = LOGITS // HALVES
-GROUPS = HALF // CLASSES
-BLOCKS = STEPS // P
+VARS = LOGITS // CLASSES
+PAIRS = 2
+HALF = LOGITS // 2
 KEEP = 0.99
 FLOOR = 0.00125
 MIX = FLOOR / KEEP
@@ -45,11 +44,11 @@ def tile_picked_ydream_kl_p_kernel(
             nc.sync.dma_start(t[:], src)
             return t
 
-        def load_scales(src, name, queue):
+        def load_scales(src, name):
             t = keep.tile([P, STORE], U8, name=name, align_bytes=64)
-            nc.vector.memset(t[:].bitcast(I32), 0)
+            nc.gpsimd.memset(t[:].bitcast(I32), 0)
             for q in range(4):
-                queue.dma_start(
+                nc.sync.dma_start(
                     out=t[32 * q : 32 * q + 4, :].bitcast(I32),
                     in_=src[0, 4 * q : 4 * q + 4, :].bitcast(I32),
                 )
@@ -60,12 +59,15 @@ def tile_picked_ydream_kl_p_kernel(
             nc.sync.dma_start(out=t[:], in_=src[0].rearrange("p n t -> p (n t)").bitcast(I32))
             return t
 
-        def load_weight(w, h, name):
-            t = keep.tile([P, PACK, HALF], F32, name=name, tag=name, align_bytes=64)
-            nc.sync.dma_start(
-                out=t[:], in_=w[:, h * HALF : (h + 1) * HALF].rearrange("(p j) c -> p j c", j=PACK)
-            )
-            return t
+        def load_weight(w, name):
+            halves = []
+            for h in range(2):
+                t = keep.tile([P, PACK, HALF], F32, name="%s%d" % (name, h), tag="%s%d" % (name, h), align_bytes=64)
+                nc.sync.dma_start(
+                    out=t[:], in_=w[:, h * HALF : (h + 1) * HALF].rearrange("(p j) c -> p j c", j=PACK)
+                )
+                halves.append(t)
+            return halves
 
         def pick_codes(words, lst, name):
             codes = keep.tile([P, STEPS], U32, name=name + "_codes", align_bytes=64)
@@ -77,178 +79,174 @@ def tile_picked_ydream_kl_p_kernel(
             nc.vector.tensor_copy(exps[:], scales[:].indirect(lst[:]))
             return exps
 
-        def interleave(raw, name):
-            grouped = keep.tile([P, HALF, PACK], BF16, name=name + "_bf", align_bytes=64)
-            nc.scalar.copy(
-                out=grouped[:].rearrange("p (c i) j -> p c j i", i=4),
-                in_=raw[:].rearrange("p j (c i) -> p c j i", i=4),
-            )
+        def interleave(halves, name):
+            grouped = keep.tile([P, LOGITS, PACK], BF16, name=name + "_bf", tag=name + "_bf", align_bytes=64)
+            for h, raw in enumerate(halves):
+                nc.scalar.copy(
+                    out=grouped[:, h * HALF : (h + 1) * HALF, :].rearrange("p (c i) j -> p c j i", i=4),
+                    in_=raw[:].rearrange("p j (c i) -> p c j i", i=4),
+                )
             return grouped
 
         def quantise(grouped, name):
-            codes = keep.tile([P, HALF], U32, name=name + "_codes", align_bytes=64)
-            exps = keep.tile([P, HALF], U8, name=name + "_exps", align_bytes=64)
+            codes = keep.tile([P, LOGITS], U32, name=name + "_codes", align_bytes=64)
+            exps = keep.tile([P, LOGITS], U8, name=name + "_exps", align_bytes=64)
             nc.vector.quantize_mx(
                 out=codes[:].bitcast(FP8X4), scales=exps[:], in_=grouped[:].rearrange("p c j -> p (c j)")
             )
             return codes, exps
 
-        def logits(pairs, name):
-            banks = []
-            for b in range(BLOCKS // 2):
-                bank = psum.tile([P, 2, HALF], F32, name=name + "_bank%d" % b, tag="logits", bufs=4)
-                for i in range(2):
-                    rows = slice((2 * b + i) * P, (2 * b + i + 1) * P)
-                    for n, ((a_codes, a_exps), (w_codes, w_exps)) in enumerate(pairs):
-                        nc.tensor.matmul_mx(
-                            out=bank[:, i, :],
-                            lhsT=a_codes[:, rows].bitcast(FP8X4),
-                            lhsT_scale=a_exps[:, rows],
-                            rhs=w_codes[:].bitcast(FP8X4),
-                            rhs_scale=w_exps[:],
-                            start=(n == 0),
-                            stop=(n == len(pairs) - 1),
-                        )
-                banks.append(bank)
-            return banks
-
-        def exp_shifted(banks, name, tag, exp_tag):
-            t = keep.tile([P, CLASSES, P], F32, name=name + "_shift", tag=tag)
-            e = keep.tile([P, CLASSES, P], F32, name=name + "_exp", tag=exp_tag, align_bytes=64)
+        def product(banks, picked, weight, start, stop):
             for b, bank in enumerate(banks):
-                top = keep.tile([P, 2 * GROUPS], F32, name=name + "_top%d" % b)
-                nc.vector.tensor_reduce(
-                    out=top[:],
-                    in_=bank[:].rearrange("p i (g d) -> p (i g) d", d=CLASSES),
-                    axis=AXIS.X,
-                    op=ALU.max,
+                rows = slice(b * P, (b + 1) * P)
+                nc.tensor.matmul_mx(
+                    out=bank[:],
+                    lhsT=picked[0][:, rows].bitcast(FP8X4),
+                    lhsT_scale=picked[1][:, rows],
+                    rhs=weight[0][:].bitcast(FP8X4),
+                    rhs_scale=weight[1][:],
+                    start=start,
+                    stop=stop,
                 )
+
+        def new_banks(name):
+            return [
+                psum.tile([P, LOGITS], F32, name="%s_bank%d" % (name, b), tag="logits", bufs=4)
+                for b in range(STEPS // P)
+            ]
+
+        def exp_shifted(banks, shift, e, name):
+            for i, bank in enumerate(banks):
+                top = keep.tile([P, VARS], F32, name="%s_top%d" % (name, i))
+                nc.vector.tensor_reduce(
+                    out=top[:], in_=bank[:].rearrange("p (g d) -> p g d", d=CLASSES), axis=AXIS.X, op=ALU.max
+                )
+                cols = slice(i * VARS, (i + 1) * VARS)
                 nc.vector.tensor_tensor(
-                    out=t[:, :, b * 2 * GROUPS : (b + 1) * 2 * GROUPS],
-                    in0=bank[:].rearrange("p i (g d) -> p d (i g)", d=CLASSES),
-                    in1=top[:].unsqueeze(1).to_broadcast([P, CLASSES, 2 * GROUPS]),
+                    out=shift[:, :, cols],
+                    in0=bank[:].rearrange("p (g d) -> p d g", d=CLASSES),
+                    in1=top[:].unsqueeze(1).to_broadcast([P, CLASSES, VARS]),
                     op=ALU.subtract,
                 )
-                cols = slice(b * 2 * GROUPS, (b + 1) * 2 * GROUPS)
-                nc.scalar.activation(out=e[:, :, cols], in_=t[:, :, cols], func=ACT.Exp)
-            return e
+                nc.scalar.activation(out=e[:, :, cols], in_=shift[:, :, cols], func=ACT.Exp)
 
-        def turn_sum(acc, parts, start, stop):
+        def turn_sum(acc, parts):
             for n, part in enumerate(parts):
                 nc.tensor.matmul(
-                    out=acc,
-                    lhsT=part,
-                    rhs=ident[:],
-                    is_transpose=True,
-                    start=start and n == 0,
-                    stop=stop and n == len(parts) - 1,
+                    out=acc, lhsT=part, rhs=ident[:], is_transpose=True, start=n == 0, stop=n == len(parts) - 1
                 )
 
-        def class_sums(e, mix_t, name, early):
-            total = psum.tile([P, P], F32, name=name + "_total", tag="total")
-            turn_sum(total[:], [e[:, d, :] for d in range(CLASSES)], True, True)
-            if early:
-                nc.scalar.activation(out=mix_t, in_=total[:], func=ACT.Copy, scale=MIX)
-            else:
-                nc.vector.tensor_scalar(out=mix_t, in0=total[:], scalar1=MIX, scalar2=None, op0=ALU.mult)
-            back = psum.tile([P, P], F32, name=name + "_back", tag="back")
+        def class_sums(e, name):
+            total = psum.tile([P, P], F32, name=name + "_total", tag="total", bufs=2)
+            turn_sum(total[:], [e[:, d, :] for d in range(CLASSES)])
+            return total
+
+        def turn_back(mix_t, name):
+            back = psum.tile([P, P], F32, name=name + "_back", tag="back", bufs=2)
             nc.tensor.transpose(back[:], mix_t, ident[:])
             return back
 
         def mixed(engine, e, addend, name):
             a = keep.tile([P, CLASSES, P], F32, name=name + "_mixed")
             engine.tensor_tensor(
-                out=a[:],
-                in0=e[:],
-                in1=addend[:].unsqueeze(1).to_broadcast([P, CLASSES, P]),
-                op=ALU.add,
+                out=a[:], in0=e, in1=addend[:].unsqueeze(1).to_broadcast([P, CLASSES, P]), op=ALU.add
             )
             return a
 
         x_list = load_list(offs, "x_list")
-        xs = load_scales(x_scales, "xs", nc.scalar)
-        wq_raw = [load_weight(wq, 0, "wq0")]
+        wq_raw = load_weight(wq, "wq")
+        xs = load_scales(x_scales, "xs")
         xw = load_words(x_words, "xw")
-        wq_raw.append(load_weight(wq, 1, "wq1"))
         e_list = load_list(obs, "e_list")
-        es = load_scales(e_scales, "es", nc.gpsimd)
+        es = load_scales(e_scales, "es")
+        wh_raw = load_weight(wh, "wh")
         ew = load_words(e_words, "ew")
-        wz_raw = [(load_weight(wh, h, "wh%d" % h), load_weight(wo, h, "wo%d" % h)) for h in range(HALVES)]
+        wo_raw = load_weight(wo, "wo")
 
         ident = keep.tile([P, P], F32, name="ident")
         make_identity(nc, ident[:])
 
-        mix = keep.tile([P, 2, HALVES, P], F32, name="mix")
+        wq_bf = interleave(wq_raw, "wq")
+        wh_bf = interleave(wh_raw, "wh")
+        wo_bf = interleave(wo_raw, "wo")
 
         x_exps = pick_scales(xs, x_list, "x")
+        wq_mx = quantise(wq_bf, "wq")
         x = (pick_codes(xw, x_list, "x"), x_exps)
         e_exps = pick_scales(es, e_list, "e")
-        wq_bf = [interleave(wq_raw[h], "wq%d" % h) for h in range(HALVES)]
-        wz_bf = [(interleave(wz_raw[h][0], "wh%d" % h), interleave(wz_raw[h][1], "wo%d" % h)) for h in range(HALVES)]
+        wh_mx = quantise(wh_bf, "wh")
+        wo_mx = quantise(wo_bf, "wo")
+        e = (pick_codes(ew, e_list, "e"), e_exps)
+
+        y_banks = new_banks("y")
+        product(y_banks, x, wq_mx, True, True)
+        y_exp = keep.tile([P, PAIRS, CLASSES, P], F32, name="y_exp", tag="wo1", align_bytes=64)
+        for u in range(PAIRS):
+            shift = keep.tile([P, CLASSES, P], F32, name="y%d_shift" % u, tag="wo_bf" if u else "wh_bf", align_bytes=64)
+            exp_shifted(y_banks[2 * u : 2 * u + 2], shift, y_exp[:, u], "y%d" % u)
+
+        z_banks = new_banks("z")
+        product(z_banks, x, wh_mx, True, False)
+        product(z_banks, e, wo_mx, False, True)
+
+        stats = keep.tile([P, 2, PAIRS, P], F32, name="stats")
         prior = []
-        for h in range(HALVES):
-            name = "y%d" % h
-            w = quantise(wq_bf[h], "wq%d" % h)
-            y_exp = exp_shifted(logits([(x, w)], name), name, name, "wo1" if h else "wq0")
-            back = class_sums(y_exp, mix[:, 0, h, :], name, True)
+        for u in range(PAIRS):
+            name = "y%d" % u
+            total = class_sums(y_exp[:, u], name)
+            nc.scalar.activation(out=stats[:, 0, u, :], in_=total[:], func=ACT.Copy, scale=MIX)
+            back = turn_back(stats[:, 0, u, :], name)
             addend = keep.tile([P, P], F32, name=name + "_addend")
             nc.scalar.copy(out=addend[:], in_=back[:])
-            prior.append(mixed(nc.gpsimd, y_exp, addend, name))
-        e = (pick_codes(ew, e_list, "e"), e_exps)
-        wz = [(quantise(wz_bf[h][0], "wh%d" % h), quantise(wz_bf[h][1], "wo%d" % h)) for h in range(HALVES)]
-        z_exp = [
-            exp_shifted(logits([(x, wz[h][0]), (e, wz[h][1])], "z%d" % h), "z%d" % h, "z%d" % h, "wh%d" % h)
-            for h in range(HALVES)
-        ]
-        post = []
-        inv = keep.tile([P, HALVES, P], F32, name="inv")
-        for h in range(HALVES):
-            back = class_sums(z_exp[h], mix[:, 1, h, :], "z%d" % h, False)
-            post.append(mixed(nc.vector, z_exp[h], back, "z%d" % h))
-        nc.vector.reciprocal(out=inv[:, 0, :], in_=mix[:, 1, 0, :])
+            prior.append(mixed(nc.gpsimd, y_exp[:, u], addend, name))
 
-        logs = keep.tile([P, 2 * HALVES * CLASSES + 2 * HALVES, P], F32, name="logs", tag="z%d" % (HALVES - 1))
+        z_exp = []
+        for u in range(PAIRS):
+            shift = keep.tile([P, CLASSES, P], F32, name="z%d_shift" % u, tag="z%d_shift" % u)
+            z_exp.append(keep.tile([P, CLASSES, P], F32, name="z%d_exp" % u))
+            exp_shifted(z_banks[2 * u : 2 * u + 2], shift, z_exp[u], "z%d" % u)
+
+        post = []
+        post_mix = stats[:, 1]
+        for u in range(PAIRS):
+            name = "z%d" % u
+            total = class_sums(z_exp[u], name)
+            nc.vector.tensor_scalar(out=post_mix[:, u, :], in0=total[:], scalar1=MIX, scalar2=None, op0=ALU.mult)
+            post.append(mixed(nc.vector, z_exp[u][:], turn_back(post_mix[:, u, :], name), name))
+
+        logs = keep.tile([P, 2 * PAIRS * CLASSES + 2 * PAIRS, P], F32, name="logs", tag="z%d_shift" % (PAIRS - 1))
         sums = []
-        for h in range(HALVES):
-            ln_b = logs[:, h * CLASSES : (h + 1) * CLASSES, :]
-            nc.scalar.activation(out=ln_b, in_=prior[h][:], func=ACT.Ln)
-            cross = keep.tile([P, CLASSES * P], F32, name="cross%d" % h)
-            nc.vector.scalar_tensor_tensor(
-                out=cross[:],
-                in0=ln_b.rearrange("p d c -> p (d c)"),
-                scalar=-1.0,
-                in1=post[h][:].rearrange("p d c -> p (d c)"),
-                op0=ALU.mult,
-                op1=ALU.mult,
-            )
-            acc = psum.tile([P, P], F32, name="acc%d" % h)
-            turn_sum(acc[:], [cross[:, d * P : (d + 1) * P] for d in range(CLASSES)], True, False)
+        for u in range(PAIRS):
+            ln_b = logs[:, u * CLASSES : (u + 1) * CLASSES, :]
+            ln_a = logs[:, (PAIRS + u) * CLASSES : (PAIRS + u + 1) * CLASSES, :]
+            gap = keep.tile([P, CLASSES, P], F32, name="gap%d" % u)
+            own = keep.tile([P, CLASSES, P], F32, name="own%d" % u)
+            parts = 2
+            for part in range(parts):
+                ds = slice(part * CLASSES // parts, (part + 1) * CLASSES // parts)
+                nc.scalar.activation(out=ln_b[:, ds], in_=prior[u][:, ds], func=ACT.Ln)
+                nc.scalar.activation(out=ln_a[:, ds], in_=post[u][:, ds], func=ACT.Ln)
+                nc.vector.tensor_tensor(out=gap[:, ds], in0=ln_a[:, ds], in1=ln_b[:, ds], op=ALU.subtract)
+                nc.vector.tensor_tensor(out=own[:, ds], in0=gap[:, ds], in1=post[u][:, ds], op=ALU.mult)
+            acc = psum.tile([P, P], F32, name="acc%d" % u, tag="logits", bufs=4)
+            turn_sum(acc[:], [own[:, d, :] for d in range(CLASSES)])
             sums.append(acc)
 
-        for h in range(HALVES):
-            ln_a = logs[:, (HALVES + h) * CLASSES : (HALVES + h + 1) * CLASSES, :]
-            own = keep.tile([P, CLASSES, P], F32, name="own%d" % h)
-            for part in range(2):
-                ds = slice(part * CLASSES // 2, (part + 1) * CLASSES // 2)
-                nc.scalar.activation(out=ln_a[:, ds], in_=post[h][:, ds], func=ACT.Ln)
-                nc.vector.tensor_tensor(out=own[:, ds], in0=ln_a[:, ds], in1=post[h][:, ds], op=ALU.mult)
-            turn_sum(sums[h][:], [own[:, d, :] for d in range(CLASSES)], False, True)
+        ln_stats = logs[:, 2 * PAIRS * CLASSES :, :]
+        nc.scalar.activation(out=ln_stats, in_=stats[:].rearrange("p s u c -> p (s u) c"), func=ACT.Ln)
+        small = keep.tile([P, 2, PAIRS, P], F32, name="small")
+        nc.scalar.activation(out=small[:, 0], in_=ln_stats[:, PAIRS:], func=ACT.Copy, scale=-1.0)
+        nc.scalar.activation(out=small[:, 1], in_=ln_stats[:, PAIRS:], func=ACT.Exp, scale=-1.0)
 
-        nc.vector.reciprocal(out=inv[:, 1, :], in_=mix[:, 1, 1, :])
-        ln_mix = logs[:, 2 * HALVES * CLASSES :, :]
-        nc.scalar.activation(out=ln_mix, in_=mix[:].rearrange("p s h c -> p (s h) c"), func=ACT.Ln)
-        gap = keep.tile([P, HALVES, P], F32, name="gap")
-        nc.gpsimd.tensor_tensor(out=gap[:], in0=ln_mix[:, :HALVES], in1=ln_mix[:, HALVES:], op=ALU.subtract)
-
-        for h in range(HALVES):
-            scaled = keep.tile([P, P], F32, name="scaled%d" % h)
+        for u in range(PAIRS):
+            scaled = keep.tile([P, P], F32, name="scaled%d" % u)
             nc.vector.scalar_tensor_tensor(
-                out=scaled[:], in0=sums[h][:], scalar=FLOOR, in1=inv[:, h, :], op0=ALU.mult, op1=ALU.mult
+                out=scaled[:], in0=sums[u][:], scalar=FLOOR, in1=small[:, 1, u, :], op0=ALU.mult, op1=ALU.mult
             )
-            res = psum.tile([P, P], F32, name="res%d" % h, tag="back" if h else "total")
-            turn_sum(res[:], [gap[:, h, :], scaled[:]], True, True)
-            staged = keep.tile([P, BLOCKS, GROUPS], F32, name="staged%d" % h)
-            nc.vector.tensor_copy(out=staged[:].rearrange("p b g -> p (b g)"), in_=res[:])
+            res = psum.tile([P, P], F32, name="res%d" % u, tag="total", bufs=2)
+            turn_sum(res[:], [ln_stats[:, u, :], small[:, 0, u, :], scaled[:]])
+            staged = keep.tile([P, 2, VARS], F32, name="staged%d" % u)
+            nc.scalar.copy(out=staged[:].rearrange("p b g -> p (b g)"), in_=res[:])
             nc.sync.dma_start(
-                out=out[:, h * GROUPS : (h + 1) * GROUPS].rearrange("(b p) g -> p b g", p=P), in_=staged[:]
+                out=out[2 * u * P : 2 * (u + 1) * P, :].rearrange("(b p) g -> p b g", p=P), in_=staged[:]
             )

@@ -44,12 +44,12 @@ def tile_picked_ydream_kl_p_kernel(
             nc.sync.dma_start(t[:], src)
             return t
 
-        def load_scales(src, name):
+        def load_scales(src, name, row):
             t = keep.tile([P, STORE], U8, name=name, align_bytes=64)
             nc.gpsimd.memset(t[:].bitcast(I32), 0)
             for q in range(4):
                 nc.sync.dma_start(
-                    out=t[32 * q : 32 * q + 4, :].bitcast(I32),
+                    out=t[32 * q + row : 32 * q + row + 4, :].bitcast(I32),
                     in_=src[0, 4 * q : 4 * q + 4, :].bitcast(I32),
                 )
             return t
@@ -82,7 +82,8 @@ def tile_picked_ydream_kl_p_kernel(
         def interleave(halves, name):
             grouped = keep.tile([P, LOGITS, PACK], BF16, name=name + "_bf", tag=name + "_bf", align_bytes=64)
             for h, raw in enumerate(halves):
-                nc.scalar.copy(
+                copy = nc.vector.tensor_copy if (name, h) in [("wq", 1), ("wo", 1)] else nc.scalar.copy
+                copy(
                     out=grouped[:, h * HALF : (h + 1) * HALF, :].rearrange("p (c i) j -> p c j i", i=4),
                     in_=raw[:].rearrange("p j (c i) -> p c j i", i=4),
                 )
@@ -111,7 +112,7 @@ def tile_picked_ydream_kl_p_kernel(
 
         def new_banks(name):
             return [
-                psum.tile([P, LOGITS], F32, name="%s_bank%d" % (name, b), tag="logits", bufs=4)
+                psum.tile([P, LOGITS], F32, name="%s_bank%d" % (name, b), tag="logits", bufs=6)
                 for b in range(STEPS // P)
             ]
 
@@ -137,28 +138,28 @@ def tile_picked_ydream_kl_p_kernel(
                 )
 
         def class_sums(e, name):
-            total = psum.tile([P, P], F32, name=name + "_total", tag="total", bufs=2)
+            total = psum.tile([P, P], F32, name=name + "_total", tag="total" if name == "y0" else "logits", bufs=1 if name == "y0" else 6)
             turn_sum(total[:], [e[:, d, :] for d in range(CLASSES)])
             return total
 
         def turn_back(mix_t, name):
-            back = psum.tile([P, P], F32, name=name + "_back", tag="back", bufs=2)
+            back = psum.tile([P, P], F32, name=name + "_back", tag="total" if name in ("z0",) else "back", bufs=1)
             nc.tensor.transpose(back[:], mix_t, ident[:])
             return back
 
         def mixed(engine, e, addend, name):
-            a = keep.tile([P, CLASSES, P], F32, name=name + "_mixed")
+            a = after_quant[:, 1] if name == "y0" else keep.tile([P, CLASSES, P], F32, name=name + "_mixed", tag=name + "_mixed")
             engine.tensor_tensor(
                 out=a[:], in0=e, in1=addend[:].unsqueeze(1).to_broadcast([P, CLASSES, P]), op=ALU.add
             )
             return a
 
         x_list = load_list(offs, "x_list")
-        wq_raw = load_weight(wq, "wq")
-        xs = load_scales(x_scales, "xs")
         xw = load_words(x_words, "xw")
+        xs = load_scales(x_scales, "xs", 0)
         e_list = load_list(obs, "e_list")
-        es = load_scales(e_scales, "es")
+        wq_raw = load_weight(wq, "wq")
+        es = load_scales(e_scales, "es", 4)
         wh_raw = load_weight(wh, "wh")
         ew = load_words(e_words, "ew")
         wo_raw = load_weight(wo, "wo")
@@ -176,43 +177,52 @@ def tile_picked_ydream_kl_p_kernel(
         e_exps = pick_scales(es, e_list, "e")
         wh_mx = quantise(wh_bf, "wh")
         wo_mx = quantise(wo_bf, "wo")
-        e = (pick_codes(ew, e_list, "e"), e_exps)
+        e = (pick_codes(ew, e_list, "e"), e_exps[4:, :])
 
         y_banks = new_banks("y")
         product(y_banks, x, wq_mx, True, True)
-        y_exp = keep.tile([P, PAIRS, CLASSES, P], F32, name="y_exp", tag="wo1", align_bytes=64)
+        after_cast = keep.tile([P, CLASSES, P], F32, name="after_cast", tag="wo0", align_bytes=64)
+        after_quant = keep.tile([P, 3, CLASSES, P], F32, name="after_quant", tag="wo_bf", align_bytes=64)
+        y_exp = [keep.tile([P, CLASSES, P], F32, name="y0_exp", tag="wh1", align_bytes=64)[:], after_cast[:, :CLASSES]]
+        y_shift = [keep.tile([P, CLASSES, P], F32, name="y0_shift")[:], after_quant[:, 0]]
         for u in range(PAIRS):
-            shift = keep.tile([P, CLASSES, P], F32, name="y%d_shift" % u, tag="wo_bf" if u else "wh_bf", align_bytes=64)
-            exp_shifted(y_banks[2 * u : 2 * u + 2], shift, y_exp[:, u], "y%d" % u)
+            exp_shifted(y_banks[2 * u : 2 * u + 2], y_shift[u], y_exp[u], "y%d" % u)
 
         z_banks = new_banks("z")
         product(z_banks, x, wh_mx, True, False)
         product(z_banks, e, wo_mx, False, True)
 
-        stats = keep.tile([P, 2, PAIRS, P], F32, name="stats")
-        prior = []
-        for u in range(PAIRS):
-            name = "y%d" % u
-            total = class_sums(y_exp[:, u], name)
-            nc.scalar.activation(out=stats[:, 0, u, :], in_=total[:], func=ACT.Copy, scale=MIX)
-            back = turn_back(stats[:, 0, u, :], name)
-            addend = keep.tile([P, P], F32, name=name + "_addend")
-            nc.scalar.copy(out=addend[:], in_=back[:])
-            prior.append(mixed(nc.gpsimd, y_exp[:, u], addend, name))
-
-        z_exp = []
-        for u in range(PAIRS):
-            shift = keep.tile([P, CLASSES, P], F32, name="z%d_shift" % u, tag="z%d_shift" % u)
-            z_exp.append(keep.tile([P, CLASSES, P], F32, name="z%d_exp" % u))
-            exp_shifted(z_banks[2 * u : 2 * u + 2], shift, z_exp[u], "z%d" % u)
-
-        post = []
+        stats = after_quant[:, 2, : 2 * PAIRS].rearrange("p (s u) c -> p s u c", s=2)
         post_mix = stats[:, 1]
-        for u in range(PAIRS):
-            name = "z%d" % u
-            total = class_sums(z_exp[u], name)
-            nc.vector.tensor_scalar(out=post_mix[:, u, :], in0=total[:], scalar1=MIX, scalar2=None, op0=ALU.mult)
-            post.append(mixed(nc.vector, z_exp[u][:], turn_back(post_mix[:, u, :], name), name))
+        z_exp = [keep.tile([P, CLASSES, P], F32, name="z%d_exp" % u)[:] for u in range(PAIRS)]
+        z_shift = [keep.tile([P, CLASSES, P], F32, name="z%d_shift" % u, tag="z%d_shift" % u)[:] for u in range(PAIRS)]
+        prior = [None, None]
+        post = [None, None]
+
+        def scale(on_vector, dst, src, factor):
+            if on_vector:
+                nc.vector.tensor_scalar(out=dst, in0=src, scalar1=factor, scalar2=None, op0=ALU.mult)
+            else:
+                nc.scalar.activation(out=dst, in_=src, func=ACT.Copy, scale=factor)
+
+        scale(False, stats[:, 0, 0, :], class_sums(y_exp[0], "y0")[:], MIX)
+        back = turn_back(stats[:, 0, 0, :], "y0")
+        addend = keep.tile([P, P], F32, name="y0_addend")
+        scale(False, addend[:], back[:], 1.0)
+        prior[0] = mixed(nc.gpsimd, y_exp[0], addend, "y0")
+        scale(False, stats[:, 0, 1, :], class_sums(y_exp[1], "y1")[:], MIX)
+        back = turn_back(stats[:, 0, 1, :], "y1")
+        addend = keep.tile([P, P], F32, name="y1_addend")
+        scale(False, addend[:], back[:], 1.0)
+        prior[1] = mixed(nc.gpsimd, y_exp[1], addend, "y1")
+        exp_shifted(z_banks[0 : 2], z_shift[0], z_exp[0], "z0")
+        exp_shifted(z_banks[2 : 4], z_shift[1], z_exp[1], "z1")
+        scale(True, post_mix[:, 0, :], class_sums(z_exp[0], "z0")[:], MIX)
+        back = turn_back(post_mix[:, 0, :], "z0")
+        post[0] = mixed(nc.vector, z_exp[0], back, "z0")
+        scale(True, post_mix[:, 1, :], class_sums(z_exp[1], "z1")[:], MIX)
+        back = turn_back(post_mix[:, 1, :], "z1")
+        post[1] = mixed(nc.vector, z_exp[1], back, "z1")
 
         logs = keep.tile([P, 2 * PAIRS * CLASSES + 2 * PAIRS, P], F32, name="logs", tag="z%d_shift" % (PAIRS - 1))
         sums = []
@@ -228,23 +238,24 @@ def tile_picked_ydream_kl_p_kernel(
                 nc.scalar.activation(out=ln_a[:, ds], in_=post[u][:, ds], func=ACT.Ln)
                 nc.vector.tensor_tensor(out=gap[:, ds], in0=ln_a[:, ds], in1=ln_b[:, ds], op=ALU.subtract)
                 nc.vector.tensor_tensor(out=own[:, ds], in0=gap[:, ds], in1=post[u][:, ds], op=ALU.mult)
-            acc = psum.tile([P, P], F32, name="acc%d" % u, tag="logits", bufs=4)
+            acc = psum.tile([P, P], F32, name="acc%d" % u, tag="logits", bufs=6)
             turn_sum(acc[:], [own[:, d, :] for d in range(CLASSES)])
             sums.append(acc)
 
         ln_stats = logs[:, 2 * PAIRS * CLASSES :, :]
         nc.scalar.activation(out=ln_stats, in_=stats[:].rearrange("p s u c -> p (s u) c"), func=ACT.Ln)
-        small = keep.tile([P, 2, PAIRS, P], F32, name="small")
-        nc.scalar.activation(out=small[:, 0], in_=ln_stats[:, PAIRS:], func=ACT.Copy, scale=-1.0)
-        nc.scalar.activation(out=small[:, 1], in_=ln_stats[:, PAIRS:], func=ACT.Exp, scale=-1.0)
+        neg = keep.tile([P, PAIRS, P], F32, name="neg")
+        inv = keep.tile([P, PAIRS, P], F32, name="inv", tag="z1_mixed")
+        nc.scalar.activation(out=neg[:], in_=ln_stats[:, PAIRS:], func=ACT.Copy, scale=-1.0)
+        nc.scalar.activation(out=inv[:], in_=ln_stats[:, PAIRS:], func=ACT.Exp, scale=-1.0)
 
         for u in range(PAIRS):
             scaled = keep.tile([P, P], F32, name="scaled%d" % u)
             nc.vector.scalar_tensor_tensor(
-                out=scaled[:], in0=sums[u][:], scalar=FLOOR, in1=small[:, 1, u, :], op0=ALU.mult, op1=ALU.mult
+                out=scaled[:], in0=sums[u][:], scalar=FLOOR, in1=inv[:, u, :], op0=ALU.mult, op1=ALU.mult
             )
-            res = psum.tile([P, P], F32, name="res%d" % u, tag="total", bufs=2)
-            turn_sum(res[:], [ln_stats[:, u, :], small[:, 0, u, :], scaled[:]])
+            res = psum.tile([P, P], F32, name="res%d" % u, tag="back" if u else "total", bufs=1)
+            turn_sum(res[:], [ln_stats[:, u, :], neg[:, u, :], scaled[:]])
             staged = keep.tile([P, 2, VARS], F32, name="staged%d" % u)
             nc.scalar.copy(out=staged[:].rearrange("p b g -> p (b g)"), in_=res[:])
             nc.sync.dma_start(

from contextlib import ExitStack

import concourse.mybir as mybir
from concourse.masks import make_identity

F32 = mybir.dt.float32
BF16 = mybir.dt.bfloat16
I32 = mybir.dt.int32
U32 = mybir.dt.uint32
U16 = mybir.dt.uint16
U8 = mybir.dt.uint8
FP8X4 = mybir.dt.float8_e4m3fn_x4
ALU = mybir.AluOpType
ACT = mybir.ActivationFunctionType
AXIS = mybir.AxisListType

P = 128
PACK = 4
K = 512
STORE = 2048
STEPS = 512
LOGITS = 512
CLASSES = 8
VARS = LOGITS // CLASSES
PAIRS = 2
HALF = LOGITS // 2
KEEP = 0.99
FLOOR = 0.00125
MIX = FLOOR / KEEP

FLOPS = 2 * 3 * STEPS * K * LOGITS


def tile_picked_ydream_kl_p_kernel(
    tc, x_words, x_scales, e_words, e_scales, wq, wh, wo, offs, obs, out
):
    nc = tc.nc
    with ExitStack() as ctx:
        keep = ctx.enter_context(tc.tile_pool(name="keep", bufs=1))
        psum = ctx.enter_context(tc.psum_pool(name="psum", bufs=1))

        def load_list(src, name):
            t = keep.tile([P, STEPS // 16], U16, name=name)
            nc.sync.dma_start(t[:], src)
            return t

        def load_scales(src, name, row):
            t = keep.tile([P, STORE], U8, name=name, align_bytes=64)
            nc.gpsimd.memset(t[:].bitcast(I32), 0)
            for q in range(4):
                nc.sync.dma_start(
                    out=t[32 * q + row : 32 * q + row + 4, :].bitcast(I32),
                    in_=src[0, 4 * q : 4 * q + 4, :].bitcast(I32),
                )
            return t

        def load_words(src, name):
            t = keep.tile([P, STORE], I32, name=name, align_bytes=64)
            nc.sync.dma_start(out=t[:], in_=src[0].rearrange("p n t -> p (n t)").bitcast(I32))
            return t

        def load_weight(w, name):
            halves = []
            for h in range(2):
                t = keep.tile([P, PACK, HALF], F32, name="%s%d" % (name, h), tag="%s%d" % (name, h), align_bytes=64)
                nc.sync.dma_start(
                    out=t[:], in_=w[:, h * HALF : (h + 1) * HALF].rearrange("(p j) c -> p j c", j=PACK)
                )
                halves.append(t)
            return halves

        def pick_codes(words, lst, name):
            codes = keep.tile([P, STEPS], U32, name=name + "_codes", align_bytes=64)
            nc.vector.tensor_copy(codes[:], words[:].bitcast(U32).indirect(lst[:]))
            return codes

        def pick_scales(scales, lst, name):
            exps = keep.tile([P, STEPS], U8, name=name + "_exps", align_bytes=64)
            nc.vector.tensor_copy(exps[:], scales[:].indirect(lst[:]))
            return exps

        def interleave(halves, name):
            grouped = keep.tile([P, LOGITS, PACK], BF16, name=name + "_bf", tag=name + "_bf", align_bytes=64)
            for h, raw in enumerate(halves):
                copy = nc.vector.tensor_copy if (name, h) in [("wq", 1), ("wo", 1)] else nc.scalar.copy
                copy(
                    out=grouped[:, h * HALF : (h + 1) * HALF, :].rearrange("p (c i) j -> p c j i", i=4),
                    in_=raw[:].rearrange("p j (c i) -> p c j i", i=4),
                )
            return grouped

        def quantise(grouped, name):
            codes = keep.tile([P, LOGITS], U32, name=name + "_codes", align_bytes=64)
            exps = keep.tile([P, LOGITS], U8, name=name + "_exps", align_bytes=64)
            nc.vector.quantize_mx(
                out=codes[:].bitcast(FP8X4), scales=exps[:], in_=grouped[:].rearrange("p c j -> p (c j)")
            )
            return codes, exps

        def product(banks, picked, weight, start, stop):
            for b, bank in enumerate(banks):
                rows = slice(b * P, (b + 1) * P)
                nc.tensor.matmul_mx(
                    out=bank[:],
                    lhsT=picked[0][:, rows].bitcast(FP8X4),
                    lhsT_scale=picked[1][:, rows],
                    rhs=weight[0][:].bitcast(FP8X4),
                    rhs_scale=weight[1][:],
                    start=start,
                    stop=stop,
                )

        def new_banks(name):
            return [
                psum.tile([P, LOGITS], F32, name="%s_bank%d" % (name, b), tag="logits", bufs=6)
                for b in range(STEPS // P)
            ]

        def exp_shifted(banks, shift, e, name):
            for i, bank in enumerate(banks):
                top = keep.tile([P, VARS], F32, name="%s_top%d" % (name, i))
                nc.vector.tensor_reduce(
                    out=top[:], in_=bank[:].rearrange("p (g d) -> p g d", d=CLASSES), axis=AXIS.X, op=ALU.max
                )
                cols = slice(i * VARS, (i + 1) * VARS)
                nc.vector.tensor_tensor(
                    out=shift[:, :, cols],
                    in0=bank[:].rearrange("p (g d) -> p d g", d=CLASSES),
                    in1=top[:].unsqueeze(1).to_broadcast([P, CLASSES, VARS]),
                    op=ALU.subtract,
                )
                nc.scalar.activation(out=e[:, :, cols], in_=shift[:, :, cols], func=ACT.Exp)

        def turn_sum(acc, parts):
            for n, part in enumerate(parts):
                nc.tensor.matmul(
                    out=acc, lhsT=part, rhs=ident[:], is_transpose=True, start=n == 0, stop=n == len(parts) - 1
                )

        def class_sums(e, name):
            total = psum.tile([P, P], F32, name=name + "_total", tag="total" if name == "y0" else "logits", bufs=1 if name == "y0" else 6)
            turn_sum(total[:], [e[:, d, :] for d in range(CLASSES)])
            return total

        def turn_back(mix_t, name):
            back = psum.tile([P, P], F32, name=name + "_back", tag="total" if name in ("z0",) else "back", bufs=1)
            nc.tensor.transpose(back[:], mix_t, ident[:])
            return back

        def mixed(engine, e, addend, name):
            a = after_quant[:, 1] if name == "y0" else keep.tile([P, CLASSES, P], F32, name=name + "_mixed", tag=name + "_mixed")
            engine.tensor_tensor(
                out=a[:], in0=e, in1=addend[:].unsqueeze(1).to_broadcast([P, CLASSES, P]), op=ALU.add
            )
            return a

        x_list = load_list(offs, "x_list")
        xw = load_words(x_words, "xw")
        xs = load_scales(x_scales, "xs", 0)
        e_list = load_list(obs, "e_list")
        wq_raw = load_weight(wq, "wq")
        es = load_scales(e_scales, "es", 4)
        wh_raw = load_weight(wh, "wh")
        ew = load_words(e_words, "ew")
        wo_raw = load_weight(wo, "wo")

        ident = keep.tile([P, P], F32, name="ident")
        make_identity(nc, ident[:])

        wq_bf = interleave(wq_raw, "wq")
        wh_bf = interleave(wh_raw, "wh")
        wo_bf = interleave(wo_raw, "wo")

        x_exps = pick_scales(xs, x_list, "x")
        wq_mx = quantise(wq_bf, "wq")
        x = (pick_codes(xw, x_list, "x"), x_exps)
        e_exps = pick_scales(es, e_list, "e")
        wh_mx = quantise(wh_bf, "wh")
        wo_mx = quantise(wo_bf, "wo")
        e = (pick_codes(ew, e_list, "e"), e_exps[4:, :])

        y_banks = new_banks("y")
        product(y_banks, x, wq_mx, True, True)
        after_cast = keep.tile([P, CLASSES, P], F32, name="after_cast", tag="wo0", align_bytes=64)
        after_quant = keep.tile([P, 3, CLASSES, P], F32, name="after_quant", tag="wo_bf", align_bytes=64)
        y_exp = [keep.tile([P, CLASSES, P], F32, name="y0_exp", tag="wh1", align_bytes=64)[:], after_cast[:, :CLASSES]]
        y_shift = [keep.tile([P, CLASSES, P], F32, name="y0_shift")[:], after_quant[:, 0]]
        for u in range(PAIRS):
            exp_shifted(y_banks[2 * u : 2 * u + 2], y_shift[u], y_exp[u], "y%d" % u)

        z_banks = new_banks("z")
        product(z_banks, x, wh_mx, True, False)
        product(z_banks, e, wo_mx, False, True)

        stats = after_quant[:, 2, : 2 * PAIRS].rearrange("p (s u) c -> p s u c", s=2)
        post_mix = stats[:, 1]
        z_exp = [keep.tile([P, CLASSES, P], F32, name="z%d_exp" % u)[:] for u in range(PAIRS)]
        z_shift = [keep.tile([P, CLASSES, P], F32, name="z%d_shift" % u, tag="z%d_shift" % u)[:] for u in range(PAIRS)]
        prior = [None, None]
        post = [None, None]

        def scale(on_vector, dst, src, factor):
            if on_vector:
                nc.vector.tensor_scalar(out=dst, in0=src, scalar1=factor, scalar2=None, op0=ALU.mult)
            else:
                nc.scalar.activation(out=dst, in_=src, func=ACT.Copy, scale=factor)

        scale(False, stats[:, 0, 0, :], class_sums(y_exp[0], "y0")[:], MIX)
        back = turn_back(stats[:, 0, 0, :], "y0")
        addend = keep.tile([P, P], F32, name="y0_addend")
        scale(False, addend[:], back[:], 1.0)
        prior[0] = mixed(nc.gpsimd, y_exp[0], addend, "y0")
        scale(False, stats[:, 0, 1, :], class_sums(y_exp[1], "y1")[:], MIX)
        back = turn_back(stats[:, 0, 1, :], "y1")
        addend = keep.tile([P, P], F32, name="y1_addend")
        scale(False, addend[:], back[:], 1.0)
        prior[1] = mixed(nc.gpsimd, y_exp[1], addend, "y1")
        exp_shifted(z_banks[0 : 2], z_shift[0], z_exp[0], "z0")
        exp_shifted(z_banks[2 : 4], z_shift[1], z_exp[1], "z1")
        scale(True, post_mix[:, 0, :], class_sums(z_exp[0], "z0")[:], MIX)
        back = turn_back(post_mix[:, 0, :], "z0")
        post[0] = mixed(nc.vector, z_exp[0], back, "z0")
        scale(True, post_mix[:, 1, :], class_sums(z_exp[1], "z1")[:], MIX)
        back = turn_back(post_mix[:, 1, :], "z1")
        post[1] = mixed(nc.vector, z_exp[1], back, "z1")

        logs = keep.tile([P, 2 * PAIRS * CLASSES + 2 * PAIRS, P], F32, name="logs", tag="z%d_shift" % (PAIRS - 1))
        sums = []
        for u in range(PAIRS):
            ln_b = logs[:, u * CLASSES : (u + 1) * CLASSES, :]
            ln_a = logs[:, (PAIRS + u) * CLASSES : (PAIRS + u + 1) * CLASSES, :]
            gap = keep.tile([P, CLASSES, P], F32, name="gap%d" % u)
            own = keep.tile([P, CLASSES, P], F32, name="own%d" % u)
            parts = 2
            for part in range(parts):
                ds = slice(part * CLASSES // parts, (part + 1) * CLASSES // parts)
                nc.scalar.activation(out=ln_b[:, ds], in_=prior[u][:, ds], func=ACT.Ln)
                nc.scalar.activation(out=ln_a[:, ds], in_=post[u][:, ds], func=ACT.Ln)
                nc.vector.tensor_tensor(out=gap[:, ds], in0=ln_a[:, ds], in1=ln_b[:, ds], op=ALU.subtract)
                nc.vector.tensor_tensor(out=own[:, ds], in0=gap[:, ds], in1=post[u][:, ds], op=ALU.mult)
            acc = psum.tile([P, P], F32, name="acc%d" % u, tag="logits", bufs=6)
            turn_sum(acc[:], [own[:, d, :] for d in range(CLASSES)])
            sums.append(acc)

        ln_stats = logs[:, 2 * PAIRS * CLASSES :, :]
        nc.scalar.activation(out=ln_stats, in_=stats[:].rearrange("p s u c -> p (s u) c"), func=ACT.Ln)
        neg = keep.tile([P, PAIRS, P], F32, name="neg")
        inv = keep.tile([P, PAIRS, P], F32, name="inv", tag="z1_mixed")
        nc.scalar.activation(out=neg[:], in_=ln_stats[:, PAIRS:], func=ACT.Copy, scale=-1.0)
        nc.scalar.activation(out=inv[:], in_=ln_stats[:, PAIRS:], func=ACT.Exp, scale=-1.0)

        for u in range(PAIRS):
            scaled = keep.tile([P, P], F32, name="scaled%d" % u)
            nc.vector.scalar_tensor_tensor(
                out=scaled[:], in0=sums[u][:], scalar=FLOOR, in1=inv[:, u, :], op0=ALU.mult, op1=ALU.mult
            )
            res = psum.tile([P, P], F32, name="res%d" % u, tag="back" if u else "total", bufs=1)
            turn_sum(res[:], [ln_stats[:, u, :], neg[:, u, :], scaled[:]])
            staged = keep.tile([P, 2, VARS], F32, name="staged%d" % u)
            nc.scalar.copy(out=staged[:].rearrange("p b g -> p (b g)"), in_=res[:])
            nc.sync.dma_start(
                out=out[2 * u * P : 2 * (u + 1) * P, :].rearrange("(b p) g -> p b g", p=P), in_=staged[:]
            )
